import numpy as np
import ml_dtypes


def mxq(x, axis, fmt="e4m3"):
    dtype, down = {"e4m3": (ml_dtypes.float8_e4m3fn, 7), "e5m2": (ml_dtypes.float8_e5m2, 14)}[fmt]
    v = np.moveaxis(np.asarray(x, np.float32).astype(ml_dtypes.bfloat16).astype(np.float64), axis, -1)
    blocks = v.reshape(v.shape[:-1] + (-1, 32))
    amax = np.abs(blocks).max(-1, keepdims=True)
    byte = np.maximum(np.where(amax > 0, np.frexp(amax)[1] - 1 + 127, 0) - down, 1)
    scale = np.exp2(byte - 127.0)
    codes = (blocks / scale).astype(np.float32).astype(dtype).astype(np.float64)
    return np.moveaxis((codes * scale).reshape(v.shape), -1, axis)


WIDE = False


def mx_kscale(k):
    if not WIDE:
        return np.ones(k)
    levels = np.array([10, -10, 5, -5, 0])
    if k % 512:
        return np.exp2(np.random.permutation(np.resize(levels, k // 32))).repeat(32)
    a = np.empty((k // 512, 16))
    for p in range(k // 512):
        a[p, :8] = np.random.permutation(np.resize(levels, 8))
        for g in range(8):
            far = levels[np.abs(levels - a[p, g]) >= 10]
            a[p, g + 8] = far[np.random.randint(len(far))]
    return np.exp2(a.ravel()).repeat(32)


def f64(x):
    return np.asarray(x).astype(np.float64)


def striped(idx):
    return np.tile(idx.reshape(-1, 16).T, (8, 1)).astype(np.uint16)


def unstriped(offs):
    return offs[:16].T.reshape(-1).astype(np.int64)


E2M1 = np.array([0.0, 0.5, 1.0, 1.5, 2.0, 3.0, 4.0, 6.0, -0.0, -0.5, -1.0, -1.5, -2.0, -3.0, -4.0, -6.0])


def pack_weight(w, fmt):
    k, n = w.shape
    w = f64(np.asarray(w, np.float32).astype(ml_dtypes.bfloat16)).reshape(k // 32, 32, n)
    amax = np.abs(w).max(1)
    if fmt == "e4m3":
        byte = np.frexp(amax)[1] - 1 + 127 - 7
    else:
        mant, ex = np.frexp(amax / 6.0)
        byte = np.where(mant > 0.5, ex, ex - 1) + 127
    byte = np.clip(np.where(amax > 0, byte, 1), 1, 254)
    scaled = (w * np.exp2(127.0 - byte)[:, None, :]).reshape(k, n).astype(np.float32)
    by_word = np.ascontiguousarray(scaled.reshape(k // 512, 128, 4, n).transpose(0, 1, 3, 2))
    if fmt == "e4m3":
        words = by_word.astype(ml_dtypes.float8_e4m3fn).view(np.uint8)
    else:
        c = by_word.astype(ml_dtypes.float4_e2m1fn).view(np.uint8) & 0xF
        words = (c[..., 0::2] | (c[..., 1::2] << 4)).reshape(k // 512, 128, 2 * n)
    return np.ascontiguousarray(words), np.ascontiguousarray(byte.astype(np.uint8).reshape(k // 512, 16, n))


def unpack_weight(words, scales, fmt):
    g, _, n = scales.shape
    words = np.ascontiguousarray(words).reshape(g, 128, n, -1)
    if fmt == "e4m3":
        vals = words.view(ml_dtypes.float8_e4m3fn).astype(np.float64)
    else:
        nib = np.empty((g, 128, n, 4), np.uint8)
        nib[..., 0::2] = words & 0xF
        nib[..., 1::2] = words >> 4
        vals = E2M1[nib]
    vals = vals * np.repeat(np.exp2(scales.astype(np.float64) - 127.0), 8, axis=1)[..., None]
    return vals.transpose(0, 1, 3, 2).reshape(g * 512, n)


def pack_table4(v):
    words, scales = pack_weight(v, "e2m1")
    g, t = words.shape[0] // 2, v.shape[1]
    words = words.reshape(g, 2, 128, t, 2).transpose(0, 2, 3, 1, 4)
    return np.concatenate([words.reshape(g, -1), scales.reshape(g, -1)], axis=1)


def unpack_table4(tab):
    g, t = tab.shape[0], tab.shape[1] // 544
    words = tab[:, :512 * t].reshape(g, 128, t, 2, 2).transpose(0, 3, 1, 2, 4).reshape(2 * g, 128, 2 * t)
    return unpack_weight(words, tab[:, 512 * t:].reshape(2 * g, 16, t), "e2m1")


K, M, T, S = 2048, 1024, 512, 256


def setup_inputs():
    n = np.random.standard_normal
    s = mx_kscale(K)[:, None]
    return {
        "tab": pack_table4(n((K, T)) * s),
        "w": (n((K, M)) / np.sqrt(K) / s).astype(np.float32),
        "offs": striped(np.random.permutation(T)[:S]),
    }


def reference(tab, w, offs):
    tab_ = unpack_table4(tab)[:, unstriped(offs)]
    w_ = mxq(f64(w), 0, "e4m3")
    y = tab_.T @ w_
    return y

@@ -1,0 +1,144 @@
+from contextlib import ExitStack
+
+import concourse.mybir as mybir
+
+K, M, T, S = 2048, 1024, 512, 256
+FLOPS = 2 * K * M * S
+
+F32 = mybir.dt.float32
+BF16 = mybir.dt.bfloat16
+I32 = mybir.dt.int32
+U32 = mybir.dt.uint32
+U16 = mybir.dt.uint16
+U8 = mybir.dt.uint8
+FP8X4 = mybir.dt.float8_e4m3fn_x4
+FP4X4 = mybir.dt.float4_e2m1fn_x4
+
+P = 128
+PACK = 4
+K_PASS = P * PACK
+PASSES = K // K_PASS
+PAIRS = PASSES // 2
+J_TILES = S // P
+WORD_BYTES = P * T * 4
+
+GROUPS = ((0, 512), (512, 256), (768, 128), (896, 128))
+BULK = ((0, 512), (512, 512))
+VECTOR_SHARE = {512: 320, 256: 160, 128: 80}
+
+
+def tile_list_tab4_tm_none_kernel(tc, tab, w, offs, out):
+    nc = tc.nc
+    with ExitStack() as ctx:
+        keep = ctx.enter_context(tc.tile_pool(name="keep", bufs=1))
+        psum = ctx.enter_context(tc.psum_pool(name="psum", bufs=1))
+
+        offsets = keep.tile([P, S // 16], U16, name="offsets")
+        words = keep.tile([P, PAIRS, T], I32, name="words", align_bytes=64)
+        planes = [keep.tile([P, 2, T], U8, name=f"planes{m}", align_bytes=64) for m in range(PAIRS)]
+        for m in range(PAIRS):
+            nc.vector.memset(planes[m][:].rearrange("p h t -> p (h t)").bitcast(I32), 0)
+
+        nc.sync.dma_start(offsets[:], offs)
+        tab32 = tab.bitcast(I32)
+        nc.sync.dma_start(
+            out=words[:],
+            in_=tab32[:, 0 : WORD_BYTES // 4].rearrange("m (p t) -> p m t", p=P),
+        )
+
+        def load_planes(m):
+            rows = tab32[m, WORD_BYTES // 4 : (WORD_BYTES + 32 * T) // 4].rearrange("(h q t) -> q h t", h=2, q=16)
+            view = planes[m][:].rearrange("p h t -> p (h t)").bitcast(I32).rearrange("p (h t) -> p h t", h=2)
+            for quad in range(4):
+                nc.sync.dma_start(out=view[32 * quad : 32 * quad + 4], in_=rows[4 * quad : 4 * quad + 4])
+
+        load_planes(0)
+        raw = []
+        for a in range(PASSES):
+            if a == 2:
+                load_planes(1)
+            pieces = [(0, M)] if a < PASSES - 1 else list(GROUPS)
+            loaded = []
+            for c0, width in pieces:
+                piece = keep.tile([P, PACK, width], F32, name=f"raw{a}_{c0}", align_bytes=64)
+                nc.sync.dma_start(
+                    out=piece[:],
+                    in_=w[a * K_PASS : (a + 1) * K_PASS, c0 : c0 + width].rearrange("(p j) c -> p j c", j=PACK),
+                )
+                loaded.append((c0, width, piece))
+            raw.append(loaded)
+
+        t_codes = [keep.tile([P, 2, 2 * S], U8, name=f"t_codes{m}", align_bytes=64) for m in range(PAIRS)]
+        t_scales = keep.tile([P, PASSES, S], U8, name="t_scales", align_bytes=64)
+        for m in range(PAIRS):
+            picked = keep.tile([P, S], U32, name=f"picked{m}", align_bytes=64)
+            nc.vector.tensor_copy(picked[:], words[:, m, :].bitcast(U32).indirect(offsets[:]))
+            nc.vector.tensor_copy(
+                out=t_codes[m][:].rearrange("p h b -> p (h b)").bitcast(U16).rearrange("p (h t) -> p h t", h=2),
+                in_=picked[:].bitcast(U16).rearrange("p (t h) -> p h t", h=2),
+            )
+            for h in range(2):
+                nc.vector.tensor_copy(t_scales[:, 2 * m + h, :], planes[m][:, h, :].indirect(offsets[:]))
+
+        grouped = [keep.tile([P, M, PACK], BF16, name=f"grouped{a}", align_bytes=64) for a in range(PASSES)]
+        w_codes = [keep.tile([P, M], U32, name=f"w_codes{a}", align_bytes=64) for a in range(PASSES)]
+        w_scales = [keep.tile([P, M], U8, name=f"w_scales{a}", align_bytes=64) for a in range(PASSES)]
+        acc = {
+            (j, c0): psum.tile([P, width], F32, name=f"acc{j}_{c0}")
+            for c0, width in GROUPS
+            for j in range(J_TILES)
+        }
+
+        def source(a, c0, width):
+            for first, span, piece in raw[a]:
+                if first <= c0 and c0 + width <= first + span:
+                    return piece[:, :, c0 - first : c0 - first + width]
+            raise ValueError("no piece holds these columns")
+
+        def cast(a, c0, width):
+            share = VECTOR_SHARE[width]
+            src = source(a, c0, width).rearrange("p j c -> p c j")
+            dst = grouped[a][:, c0 : c0 + width, :]
+            nc.vector.tensor_copy(out=dst[:, :share, :], in_=src[:, :share, :])
+            nc.scalar.copy(out=dst[:, share:, :], in_=src[:, share:, :])
+
+        def quantise(a, c0, width):
+            cols = slice(c0, c0 + width)
+            nc.vector.quantize_mx(
+                out=w_codes[a][:, cols].bitcast(FP8X4),
+                scales=w_scales[a][:, cols],
+                in_=grouped[a][:, cols, :].rearrange("p c j -> p (c j)"),
+            )
+
+        def multiply(a, c0, width):
+            step = 512 if width == 512 else 128
+            for j in range(J_TILES):
+                for n in range(0, width, step):
+                    cols = slice(c0 + n, c0 + n + step)
+                    nc.tensor.matmul_mx(
+                        out=acc[j, c0][:, n : n + step],
+                        lhsT=t_codes[a // 2][:, a % 2, 2 * P * j : 2 * P * (j + 1)].bitcast(FP4X4),
+                        lhsT_scale=t_scales[:, a, P * j : P * (j + 1)],
+                        rhs=w_codes[a][:, cols].bitcast(FP8X4),
+                        rhs_scale=w_scales[a][:, cols],
+                        start=(a == 0 and n == 0),
+                        stop=(a == PASSES - 1 and n + step == width),
+                    )
+
+        for a in range(PASSES - 1):
+            for c0, width in BULK:
+                cast(a, c0, width)
+            for c0, width in BULK:
+                quantise(a, c0, width)
+            for c0, width in GROUPS:
+                multiply(a, c0, width)
+
+        out_view = out.rearrange("(j p) n -> p j n", p=P)
+        for c0, width in GROUPS:
+            cast(PASSES - 1, c0, width)
+            quantise(PASSES - 1, c0, width)
+            multiply(PASSES - 1, c0, width)
+            result = keep.tile([P, J_TILES, width], F32, name=f"result{c0}", align_bytes=64)
+            nc.vector.tensor_copy(out=result[:, 0, :], in_=acc[0, c0][:])
+            nc.scalar.copy(out=result[:, 1, :], in_=acc[1, c0][:])
+            nc.sync.dma_start(out=out_view[:, :, c0 : c0 + width], in_=result[:])

@@ -22,9 +22,17 @@ PAIRS = PASSES // 2
 J_TILES = S // P
 WORD_BYTES = P * T * 4
 
-GROUPS = ((0, 512), (512, 256), (768, 128), (896, 128))
-BULK = ((0, 512), (512, 512))
-VECTOR_SHARE = {512: 320, 256: 160, 128: 80}
+GROUPS = ((0, 512), (512, 256), (768, 256))
+PLAN = (
+    (0, 0, 1024),
+    (1, 0, 1024),
+    (2, 0, 512),
+    (3, 0, 512),
+    (2, 512, 512),
+    (3, 512, 256),
+    (3, 768, 256),
+)
+VECTOR_SHARE = {256: 160, 512: 304}
 
 
 def tile_list_tab4_tm_none_kernel(tc, tab, w, offs, out):
@@ -54,23 +62,19 @@ def tile_list_tab4_tm_none_kernel(tc, tab, w, offs, out):
 
         load_planes(0)
         raw = []
-        for a in range(PASSES):
-            if a == 2:
+        for step, (a, c0, width) in enumerate(PLAN):
+            if step == 1:
                 load_planes(1)
-            pieces = [(0, M)] if a < PASSES - 1 else list(GROUPS)
-            loaded = []
-            for c0, width in pieces:
-                piece = keep.tile([P, PACK, width], F32, name=f"raw{a}_{c0}", align_bytes=64)
-                nc.sync.dma_start(
-                    out=piece[:],
-                    in_=w[a * K_PASS : (a + 1) * K_PASS, c0 : c0 + width].rearrange("(p j) c -> p j c", j=PACK),
-                )
-                loaded.append((c0, width, piece))
-            raw.append(loaded)
+            piece = keep.tile([P, PACK, width], F32, name=f"raw{a}_{c0}", align_bytes=64)
+            nc.sync.dma_start(
+                out=piece[:],
+                in_=w[a * K_PASS : (a + 1) * K_PASS, c0 : c0 + width].rearrange("(p j) c -> p j c", j=PACK),
+            )
+            raw.append(piece)
 
         t_codes = [keep.tile([P, 2, 2 * S], U8, name=f"t_codes{m}", align_bytes=64) for m in range(PAIRS)]
         t_scales = keep.tile([P, PASSES, S], U8, name="t_scales", align_bytes=64)
-        for m in range(PAIRS):
+        def gather(m):
             picked = keep.tile([P, S], U32, name=f"picked{m}", align_bytes=64)
             nc.vector.tensor_copy(picked[:], words[:, m, :].bitcast(U32).indirect(offsets[:]))
             nc.vector.tensor_copy(
@@ -80,6 +84,7 @@ def tile_list_tab4_tm_none_kernel(tc, tab, w, offs, out):
             for h in range(2):
                 nc.vector.tensor_copy(t_scales[:, 2 * m + h, :], planes[m][:, h, :].indirect(offsets[:]))
 
+        gather(0)
         grouped = [keep.tile([P, M, PACK], BF16, name=f"grouped{a}", align_bytes=64) for a in range(PASSES)]
         w_codes = [keep.tile([P, M], U32, name=f"w_codes{a}", align_bytes=64) for a in range(PASSES)]
         w_scales = [keep.tile([P, M], U8, name=f"w_scales{a}", align_bytes=64) for a in range(PASSES)]
@@ -89,18 +94,14 @@ def tile_list_tab4_tm_none_kernel(tc, tab, w, offs, out):
             for j in range(J_TILES)
         }
 
-        def source(a, c0, width):
-            for first, span, piece in raw[a]:
-                if first <= c0 and c0 + width <= first + span:
-                    return piece[:, :, c0 - first : c0 - first + width]
-            raise ValueError("no piece holds these columns")
-
-        def cast(a, c0, width):
+        def cast(a, c0, width, src):
             share = VECTOR_SHARE[width]
-            src = source(a, c0, width).rearrange("p j c -> p c j")
             dst = grouped[a][:, c0 : c0 + width, :]
-            nc.vector.tensor_copy(out=dst[:, :share, :], in_=src[:, :share, :])
-            nc.scalar.copy(out=dst[:, share:, :], in_=src[:, share:, :])
+            for copy, cols in ((nc.vector.tensor_copy, slice(0, share)), (nc.scalar.copy, slice(share, width))):
+                copy(
+                    out=dst[:, cols, :].rearrange("p (c i) j -> p c j i", i=4),
+                    in_=src[:, :, cols].rearrange("p j (c i) -> p c j i", i=4),
+                )
 
         def quantise(a, c0, width):
             cols = slice(c0, c0 + width)
@@ -125,20 +126,33 @@ def tile_list_tab4_tm_none_kernel(tc, tab, w, offs, out):
                         stop=(a == PASSES - 1 and n + step == width),
                     )
 
-        for a in range(PASSES - 1):
-            for c0, width in BULK:
-                cast(a, c0, width)
-            for c0, width in BULK:
-                quantise(a, c0, width)
-            for c0, width in GROUPS:
-                multiply(a, c0, width)
-
         out_view = out.rearrange("(j p) n -> p j n", p=P)
-        for c0, width in GROUPS:
-            cast(PASSES - 1, c0, width)
-            quantise(PASSES - 1, c0, width)
-            multiply(PASSES - 1, c0, width)
+
+        def finish(c0, width):
             result = keep.tile([P, J_TILES, width], F32, name=f"result{c0}", align_bytes=64)
-            nc.vector.tensor_copy(out=result[:, 0, :], in_=acc[0, c0][:])
+            if c0 == GROUPS[-1][0]:
+                nc.vector.tensor_copy(out=result[:, 0, :], in_=acc[0, c0][:])
+            else:
+                nc.scalar.copy(out=result[:, 0, :], in_=acc[0, c0][:])
             nc.scalar.copy(out=result[:, 1, :], in_=acc[1, c0][:])
             nc.sync.dma_start(out=out_view[:, :, c0 : c0 + width], in_=result[:])
+
+        waiting = []
+        for step, (piece, (a, c0, width)) in enumerate(zip(raw, PLAN)):
+            if step == 1:
+                gather(1)
+            parts = [(c, min(width, 512)) for c in range(0, width, 512)]
+            for c, n in parts:
+                cast(a, c0 + c, n, piece[:, :, c : c + n])
+            for c, n in parts:
+                quantise(a, c0 + c, n)
+            done = [g for g in GROUPS if c0 <= g[0] < c0 + width]
+            for first, span in done:
+                multiply(a, first, span)
+            waiting.append(done if a == PASSES - 1 else [])
+            if len(waiting) > 2:
+                for group in waiting.pop(0):
+                    finish(*group)
+        for groups in waiting:
+            for group in groups:
+                finish(*group)

@@ -23,16 +23,16 @@ J_TILES = S // P
 WORD_BYTES = P * T * 4
 
 GROUPS = ((0, 512), (512, 256), (768, 256))
+PARTS = (((0, 1024),), ((0, 1024),), ((0, 512), (512, 512)))
 PLAN = (
     (0, 0, 1024),
     (1, 0, 1024),
-    (2, 0, 512),
+    (2, 0, 1024),
     (3, 0, 512),
-    (2, 512, 512),
     (3, 512, 256),
     (3, 768, 256),
 )
-VECTOR_SHARE = {256: 160, 512: 304}
+VECTOR_SHARE = {256: 160, 512: 272, 1024: 512}
 
 
 def tile_list_tab4_tm_none_kernel(tc, tab, w, offs, out):
@@ -81,10 +81,14 @@ def tile_list_tab4_tm_none_kernel(tc, tab, w, offs, out):
                 out=t_codes[m][:].rearrange("p h b -> p (h b)").bitcast(U16).rearrange("p (h t) -> p h t", h=2),
                 in_=picked[:].bitcast(U16).rearrange("p (t h) -> p h t", h=2),
             )
+
+        def gather_scales(m):
             for h in range(2):
                 nc.vector.tensor_copy(t_scales[:, 2 * m + h, :], planes[m][:, h, :].indirect(offsets[:]))
 
         gather(0)
+        gather_scales(0)
+        gather(1)
         grouped = [keep.tile([P, M, PACK], BF16, name=f"grouped{a}", align_bytes=64) for a in range(PASSES)]
         w_codes = [keep.tile([P, M], U32, name=f"w_codes{a}", align_bytes=64) for a in range(PASSES)]
         w_scales = [keep.tile([P, M], U8, name=f"w_scales{a}", align_bytes=64) for a in range(PASSES)]
@@ -94,7 +98,9 @@ def tile_list_tab4_tm_none_kernel(tc, tab, w, offs, out):
             for j in range(J_TILES)
         }
 
-        def cast(a, c0, width, src):
+        def cast(a, c0, width):
+            first, piece = [(f, t) for (b, f, n), t in zip(PLAN, raw) if b == a and f <= c0 < f + n][0]
+            src = piece[:, :, c0 - first : c0 - first + width]
             share = VECTOR_SHARE[width]
             dst = grouped[a][:, c0 : c0 + width, :]
             for copy, cols in ((nc.vector.tensor_copy, slice(0, share)), (nc.scalar.copy, slice(share, width))):
@@ -130,29 +136,27 @@ def tile_list_tab4_tm_none_kernel(tc, tab, w, offs, out):
 
         def finish(c0, width):
             result = keep.tile([P, J_TILES, width], F32, name=f"result{c0}", align_bytes=64)
-            if c0 == GROUPS[-1][0]:
+            if c0 in (0, 768):
                 nc.vector.tensor_copy(out=result[:, 0, :], in_=acc[0, c0][:])
             else:
                 nc.scalar.copy(out=result[:, 0, :], in_=acc[0, c0][:])
             nc.scalar.copy(out=result[:, 1, :], in_=acc[1, c0][:])
             nc.sync.dma_start(out=out_view[:, :, c0 : c0 + width], in_=result[:])
 
-        waiting = []
-        for step, (piece, (a, c0, width)) in enumerate(zip(raw, PLAN)):
-            if step == 1:
-                gather(1)
-            parts = [(c, min(width, 512)) for c in range(0, width, 512)]
-            for c, n in parts:
-                cast(a, c0 + c, n, piece[:, :, c : c + n])
-            for c, n in parts:
-                quantise(a, c0 + c, n)
-            done = [g for g in GROUPS if c0 <= g[0] < c0 + width]
-            for first, span in done:
-                multiply(a, first, span)
-            waiting.append(done if a == PASSES - 1 else [])
-            if len(waiting) > 2:
-                for group in waiting.pop(0):
-                    finish(*group)
-        for groups in waiting:
-            for group in groups:
-                finish(*group)
+        for a in range(PASSES - 1):
+            if a == 1:
+                gather_scales(1)
+            for c0, width in PARTS[a]:
+                cast(a, c0, width)
+            for c0, width in PARTS[a]:
+                quantise(a, c0, width)
+            for c0, width in GROUPS:
+                multiply(a, c0, width)
+        for g, (c0, width) in enumerate(GROUPS):
+            cast(PASSES - 1, c0, width)
+            quantise(PASSES - 1, c0, width)
+            multiply(PASSES - 1, c0, width)
+            if g >= 1:
+                finish(*GROUPS[g - 1])
+        for g in range(len(GROUPS) - 1, len(GROUPS)):
+            finish(*GROUPS[g])

from contextlib import ExitStack

import concourse.mybir as mybir

K, M, T, S = 2048, 1024, 512, 256
FLOPS = 2 * K * M * S

F32 = mybir.dt.float32
BF16 = mybir.dt.bfloat16
I32 = mybir.dt.int32
U32 = mybir.dt.uint32
U16 = mybir.dt.uint16
U8 = mybir.dt.uint8
FP8X4 = mybir.dt.float8_e4m3fn_x4
FP4X4 = mybir.dt.float4_e2m1fn_x4

P = 128
PACK = 4
K_PASS = P * PACK
PASSES = K // K_PASS
PAIRS = PASSES // 2
J_TILES = S // P
WORD_BYTES = P * T * 4

GROUPS = ((0, 512), (512, 256), (768, 256))
PARTS = (((0, 1024),), ((0, 1024),), ((0, 512), (512, 512)))
PLAN = (
    (0, 0, 1024),
    (1, 0, 1024),
    (2, 0, 1024),
    (3, 0, 512),
    (3, 512, 256),
    (3, 768, 256),
)
VECTOR_SHARE = {256: 160, 512: 272, 1024: 512}


def tile_list_tab4_tm_none_kernel(tc, tab, w, offs, out):
    nc = tc.nc
    with ExitStack() as ctx:
        keep = ctx.enter_context(tc.tile_pool(name="keep", bufs=1))
        psum = ctx.enter_context(tc.psum_pool(name="psum", bufs=1))

        offsets = keep.tile([P, S // 16], U16, name="offsets")
        words = keep.tile([P, PAIRS, T], I32, name="words", align_bytes=64)
        planes = [keep.tile([P, 2, T], U8, name=f"planes{m}", align_bytes=64) for m in range(PAIRS)]
        for m in range(PAIRS):
            nc.vector.memset(planes[m][:].rearrange("p h t -> p (h t)").bitcast(I32), 0)

        nc.sync.dma_start(offsets[:], offs)
        tab32 = tab.bitcast(I32)
        nc.sync.dma_start(
            out=words[:],
            in_=tab32[:, 0 : WORD_BYTES // 4].rearrange("m (p t) -> p m t", p=P),
        )

        def load_planes(m):
            rows = tab32[m, WORD_BYTES // 4 : (WORD_BYTES + 32 * T) // 4].rearrange("(h q t) -> q h t", h=2, q=16)
            view = planes[m][:].rearrange("p h t -> p (h t)").bitcast(I32).rearrange("p (h t) -> p h t", h=2)
            for quad in range(4):
                nc.sync.dma_start(out=view[32 * quad : 32 * quad + 4], in_=rows[4 * quad : 4 * quad + 4])

        load_planes(0)
        raw = []
        for step, (a, c0, width) in enumerate(PLAN):
            if step == 1:
                load_planes(1)
            piece = keep.tile([P, PACK, width], F32, name=f"raw{a}_{c0}", align_bytes=64)
            nc.sync.dma_start(
                out=piece[:],
                in_=w[a * K_PASS : (a + 1) * K_PASS, c0 : c0 + width].rearrange("(p j) c -> p j c", j=PACK),
            )
            raw.append(piece)

        t_codes = [keep.tile([P, 2, 2 * S], U8, name=f"t_codes{m}", align_bytes=64) for m in range(PAIRS)]
        t_scales = keep.tile([P, PASSES, S], U8, name="t_scales", align_bytes=64)
        def gather(m):
            picked = keep.tile([P, S], U32, name=f"picked{m}", align_bytes=64)
            nc.vector.tensor_copy(picked[:], words[:, m, :].bitcast(U32).indirect(offsets[:]))
            nc.vector.tensor_copy(
                out=t_codes[m][:].rearrange("p h b -> p (h b)").bitcast(U16).rearrange("p (h t) -> p h t", h=2),
                in_=picked[:].bitcast(U16).rearrange("p (t h) -> p h t", h=2),
            )

        def gather_scales(m):
            for h in range(2):
                nc.vector.tensor_copy(t_scales[:, 2 * m + h, :], planes[m][:, h, :].indirect(offsets[:]))

        gather(0)
        gather_scales(0)
        gather(1)
        grouped = [keep.tile([P, M, PACK], BF16, name=f"grouped{a}", align_bytes=64) for a in range(PASSES)]
        w_codes = [keep.tile([P, M], U32, name=f"w_codes{a}", align_bytes=64) for a in range(PASSES)]
        w_scales = [keep.tile([P, M], U8, name=f"w_scales{a}", align_bytes=64) for a in range(PASSES)]
        acc = {
            (j, c0): psum.tile([P, width], F32, name=f"acc{j}_{c0}")
            for c0, width in GROUPS
            for j in range(J_TILES)
        }

        def cast(a, c0, width):
            first, piece = [(f, t) for (b, f, n), t in zip(PLAN, raw) if b == a and f <= c0 < f + n][0]
            src = piece[:, :, c0 - first : c0 - first + width]
            share = VECTOR_SHARE[width]
            dst = grouped[a][:, c0 : c0 + width, :]
            for copy, cols in ((nc.vector.tensor_copy, slice(0, share)), (nc.scalar.copy, slice(share, width))):
                copy(
                    out=dst[:, cols, :].rearrange("p (c i) j -> p c j i", i=4),
                    in_=src[:, :, cols].rearrange("p j (c i) -> p c j i", i=4),
                )

        def quantise(a, c0, width):
            cols = slice(c0, c0 + width)
            nc.vector.quantize_mx(
                out=w_codes[a][:, cols].bitcast(FP8X4),
                scales=w_scales[a][:, cols],
                in_=grouped[a][:, cols, :].rearrange("p c j -> p (c j)"),
            )

        def multiply(a, c0, width):
            step = 512 if width == 512 else 128
            for j in range(J_TILES):
                for n in range(0, width, step):
                    cols = slice(c0 + n, c0 + n + step)
                    nc.tensor.matmul_mx(
                        out=acc[j, c0][:, n : n + step],
                        lhsT=t_codes[a // 2][:, a % 2, 2 * P * j : 2 * P * (j + 1)].bitcast(FP4X4),
                        lhsT_scale=t_scales[:, a, P * j : P * (j + 1)],
                        rhs=w_codes[a][:, cols].bitcast(FP8X4),
                        rhs_scale=w_scales[a][:, cols],
                        start=(a == 0 and n == 0),
                        stop=(a == PASSES - 1 and n + step == width),
                    )

        out_view = out.rearrange("(j p) n -> p j n", p=P)

        def finish(c0, width):
            result = keep.tile([P, J_TILES, width], F32, name=f"result{c0}", align_bytes=64)
            if c0 in (0, 768):
                nc.vector.tensor_copy(out=result[:, 0, :], in_=acc[0, c0][:])
            else:
                nc.scalar.copy(out=result[:, 0, :], in_=acc[0, c0][:])
            nc.scalar.copy(out=result[:, 1, :], in_=acc[1, c0][:])
            nc.sync.dma_start(out=out_view[:, :, c0 : c0 + width], in_=result[:])

        for a in range(PASSES - 1):
            if a == 1:
                gather_scales(1)
            for c0, width in PARTS[a]:
                cast(a, c0, width)
            for c0, width in PARTS[a]:
                quantise(a, c0, width)
            for c0, width in GROUPS:
                multiply(a, c0, width)
        for g, (c0, width) in enumerate(GROUPS):
            cast(PASSES - 1, c0, width)
            quantise(PASSES - 1, c0, width)
            multiply(PASSES - 1, c0, width)
            if g >= 1:
                finish(*GROUPS[g - 1])
        for g in range(len(GROUPS) - 1, len(GROUPS)):
            finish(*GROUPS[g])
